import numpy as np
import ml_dtypes


def mxq(x, axis, fmt="e4m3"):
    dtype, down = {"e4m3": (ml_dtypes.float8_e4m3fn, 7), "e5m2": (ml_dtypes.float8_e5m2, 14)}[fmt]
    v = np.moveaxis(np.asarray(x, np.float32).astype(ml_dtypes.bfloat16).astype(np.float64), axis, -1)
    blocks = v.reshape(v.shape[:-1] + (-1, 32))
    amax = np.abs(blocks).max(-1, keepdims=True)
    byte = np.maximum(np.where(amax > 0, np.frexp(amax)[1] - 1 + 127, 0) - down, 1)
    scale = np.exp2(byte - 127.0)
    codes = (blocks / scale).astype(np.float32).astype(dtype).astype(np.float64)
    return np.moveaxis((codes * scale).reshape(v.shape), -1, axis)


WIDE = False


def mx_kscale(k):
    if not WIDE:
        return np.ones(k)
    levels = np.array([10, -10, 5, -5, 0])
    if k % 512:
        return np.exp2(np.random.permutation(np.resize(levels, k // 32))).repeat(32)
    a = np.empty((k // 512, 16))
    for p in range(k // 512):
        a[p, :8] = np.random.permutation(np.resize(levels, 8))
        for g in range(8):
            far = levels[np.abs(levels - a[p, g]) >= 10]
            a[p, g + 8] = far[np.random.randint(len(far))]
    return np.exp2(a.ravel()).repeat(32)


def f64(x):
    return np.asarray(x).astype(np.float64)


def striped(idx):
    return np.tile(idx.reshape(-1, 16).T, (8, 1)).astype(np.uint16)


def unstriped(offs):
    return offs[:16].T.reshape(-1).astype(np.int64)


E2M1 = np.array([0.0, 0.5, 1.0, 1.5, 2.0, 3.0, 4.0, 6.0, -0.0, -0.5, -1.0, -1.5, -2.0, -3.0, -4.0, -6.0])


def pack_weight(w, fmt):
    k, n = w.shape
    w = f64(np.asarray(w, np.float32).astype(ml_dtypes.bfloat16)).reshape(k // 32, 32, n)
    amax = np.abs(w).max(1)
    if fmt == "e4m3":
        byte = np.frexp(amax)[1] - 1 + 127 - 7
    else:
        mant, ex = np.frexp(amax / 6.0)
        byte = np.where(mant > 0.5, ex, ex - 1) + 127
    byte = np.clip(np.where(amax > 0, byte, 1), 1, 254)
    scaled = (w * np.exp2(127.0 - byte)[:, None, :]).reshape(k, n).astype(np.float32)
    by_word = np.ascontiguousarray(scaled.reshape(k // 512, 128, 4, n).transpose(0, 1, 3, 2))
    if fmt == "e4m3":
        words = by_word.astype(ml_dtypes.float8_e4m3fn).view(np.uint8)
    else:
        c = by_word.astype(ml_dtypes.float4_e2m1fn).view(np.uint8) & 0xF
        words = (c[..., 0::2] | (c[..., 1::2] << 4)).reshape(k // 512, 128, 2 * n)
    return np.ascontiguousarray(words), np.ascontiguousarray(byte.astype(np.uint8).reshape(k // 512, 16, n))


def unpack_weight(words, scales, fmt):
    g, _, n = scales.shape
    words = np.ascontiguousarray(words).reshape(g, 128, n, -1)
    if fmt == "e4m3":
        vals = words.view(ml_dtypes.float8_e4m3fn).astype(np.float64)
    else:
        nib = np.empty((g, 128, n, 4), np.uint8)
        nib[..., 0::2] = words & 0xF
        nib[..., 1::2] = words >> 4
        vals = E2M1[nib]
    vals = vals * np.repeat(np.exp2(scales.astype(np.float64) - 127.0), 8, axis=1)[..., None]
    return vals.transpose(0, 1, 3, 2).reshape(g * 512, n)


def silu(v):
    return v / (1.0 + np.exp(-np.maximum(v, -700.0)))


K, T, E, H, N = 1024, 512, 2, 512, 384
COUNTS = (128, 384)
STARTS = np.cumsum((0,) + COUNTS)


def by_expert(wq, xq):
    return np.concatenate([wq[e].T @ xq[:, STARTS[e]:STARTS[e + 1]] for e in range(E)], axis=1)


def setup_inputs():
    n = np.random.standard_normal
    s = mx_kscale(K)[:, None]
    u = mx_kscale(H)
    expert = np.random.permutation(np.repeat(np.arange(E), COUNTS))
    slot_token = np.argsort(expert, kind="stable")
    w1 = [pack_weight(m, "e2m1") for m in n((E, K, H)) / np.sqrt(K) / s[None]]
    w3 = [pack_weight(m, "e2m1") for m in n((E, K, H)) / np.sqrt(K) / s[None] * u[None, None, :]]
    w2 = [pack_weight(m, "e2m1") for m in n((E, H, N)) / np.sqrt(H) / u[None, :, None]]
    return {
        "xT": (n((K, T)) * s).astype(np.float32),
        "w1_words": np.stack([m[0] for m in w1]),
        "w1_scales": np.stack([m[1] for m in w1]),
        "w3_words": np.stack([m[0] for m in w3]),
        "w3_scales": np.stack([m[1] for m in w3]),
        "w2_words": np.stack([m[0] for m in w2]),
        "w2_scales": np.stack([m[1] for m in w2]),
        "gate": np.tile(np.random.uniform(0.2, 1.0, T), (N, 1)).astype(np.float32),
        "offs": striped(slot_token),
    }


def reference(xT, w1_words, w1_scales, w3_words, w3_scales, w2_words, w2_scales, gate, offs):
    idx = unstriped(offs)
    w1 = np.stack([unpack_weight(w1_words[e], w1_scales[e], "e2m1") for e in range(E)])
    w3 = np.stack([unpack_weight(w3_words[e], w3_scales[e], "e2m1") for e in range(E)])
    w2 = np.stack([unpack_weight(w2_words[e], w2_scales[e], "e2m1") for e in range(E)])
    xq = mxq(f64(xT)[:, idx], 0, "e4m3")
    h = silu(by_expert(w1, xq))
    h = h * by_expert(w3, xq)
    y = by_expert(w2, mxq(h, 0, "e4m3"))
    out = np.zeros((N, T))
    out[:, idx] = f64(gate) * y
    return out

@@ -1,0 +1,190 @@
+from contextlib import ExitStack
+
+import concourse.mybir as mybir
+from concourse.masks import make_identity
+
+K, T, E, H, N = 1024, 512, 2, 512, 384
+COUNTS = (128, 384)
+STARTS = (0, 128)
+
+F32 = mybir.dt.float32
+BF16 = mybir.dt.bfloat16
+I32 = mybir.dt.int32
+U32 = mybir.dt.uint32
+U16 = mybir.dt.uint16
+U8 = mybir.dt.uint8
+FP8X4 = mybir.dt.float8_e4m3fn_x4
+FP4X4 = mybir.dt.float4_e2m1fn_x4
+ACT = mybir.ActivationFunctionType
+MULT = mybir.AluOpType.mult
+
+P = 128
+PASSES = K // 512
+HALF = T // 2
+TILES = T // P
+N_TILES = N // P
+
+FLOPS = 2 * T * (2 * K * H + H * N)
+BYTES = 4 * K * T + 2 * E * (K * H // 2 + K * H // 32) + E * (H * N // 2 + H * N // 32) + 4 * P * T + 2 * P * (T // 16) + 4 * N * T
+
+
+def tile_moe_rag_glu_silu_kernel(
+    tc, xT, w1_words, w1_scales, w3_words, w3_scales, w2_words, w2_scales, gate, offs, out
+):
+    nc = tc.nc
+    with ExitStack() as ctx:
+        keep = ctx.enter_context(tc.tile_pool(name="keep", bufs=1))
+        work = ctx.enter_context(tc.tile_pool(name="work", bufs=2))
+        psum_ab = ctx.enter_context(tc.psum_pool(name="psum_ab", bufs=3))
+        psum_one = ctx.enter_context(tc.psum_pool(name="psum_one", bufs=1))
+
+        offsets = keep.tile([P, T // 16], U16, name="offsets")
+        nc.sync.dma_start(offsets[:], offs)
+
+        all_bytes = []
+        for s in range(PASSES):
+            plane = keep.tile([P, T], U8, name=f"all_bytes_{s}", align_bytes=64)
+            nc.gpsimd.memset(plane[:], 0)
+            all_bytes.append(plane)
+
+        x_raw = {}
+
+        def load_x(s):
+            rows = xT[s * 512 : (s + 1) * 512, :].rearrange("(p j) w -> p j w", j=4)
+            for half in range(2):
+                raw = keep.tile([P, 4, HALF], F32, name=f"x_raw_{s}_{half}")
+                nc.sync.dma_start(raw[:], rows[:, :, half * HALF : (half + 1) * HALF])
+                x_raw[s, half] = raw
+
+        def load_scales(name, scales):
+            passes, width = scales.shape[1], scales.shape[3]
+            plane = keep.tile([P, E * passes, width], U8, name=f"{name}_plane", align_bytes=64)
+            nc.vector.memset(plane[:].bitcast(I32), 0)
+            rows = scales.bitcast(I32).rearrange("e s q i -> q (e s) i")
+            for q in range(4):
+                nc.sync.dma_start(plane[32 * q : 32 * q + 4, :, :].bitcast(I32), rows[4 * q : 4 * q + 4, :, :])
+            return plane
+
+        def load_words(name, words):
+            passes, width = words.shape[1], words.shape[3]
+            codes = keep.tile([P, E * passes, width], U8, name=f"{name}_codes", align_bytes=64)
+            nc.sync.dma_start(codes[:].bitcast(I32), words.bitcast(I32).rearrange("e s p b -> p (e s) b"))
+            return codes
+
+        load_x(0)
+        w1_sc = load_scales("w1", w1_scales)
+        load_x(1)
+        w3_sc = load_scales("w3", w3_scales)
+        w1 = load_words("w1", w1_words)
+        w3 = load_words("w3", w3_words)
+        w2_sc = load_scales("w2", w2_scales)
+        w2 = load_words("w2", w2_words)
+
+        gate_sb = keep.tile([P, T], F32, name="gate_sb")
+        nc.sync.dma_start(gate_sb[:], gate[0:P, :])
+
+        ident = keep.tile([P, P], F32, name="ident")
+        make_identity(nc, ident[:])
+
+        warm = keep.tile([P, 1], F32, name="warm")
+        nc.vector.memset(warm[:], 0.0)
+        warm_out = keep.tile([P, 1], F32, name="warm_out")
+        nc.scalar.activation(warm_out[:], warm[:], ACT.Silu)
+
+        x_words, x_bytes = [], []
+        for s in range(PASSES):
+            words = keep.tile([P, T], U32, name=f"all_words_{s}", align_bytes=64)
+            for half in range(2):
+                grouped = keep.tile([P, HALF, 4], BF16, name=f"x_grouped_{s}_{half}", align_bytes=64)
+                src = x_raw[s, half][:].rearrange("p j w -> p w j")
+                if half == 0:
+                    nc.scalar.copy(grouped[:], src)
+                else:
+                    nc.vector.tensor_copy(grouped[:], src)
+                cols = slice(half * HALF, (half + 1) * HALF)
+                nc.vector.quantize_mx(
+                    out=words[:, cols].bitcast(FP8X4),
+                    scales=all_bytes[s][:, cols],
+                    in_=grouped[:].rearrange("p w j -> p (w j)"),
+                )
+            slot_words = keep.tile([P, T], U32, name=f"slot_words_{s}", align_bytes=64)
+            slot_bytes = keep.tile([P, T], U8, name=f"slot_bytes_{s}", align_bytes=64)
+            for e in range(E):
+                lo, hi = STARTS[e], STARTS[e] + COUNTS[e]
+                where = offsets[:, lo // 16 : hi // 16]
+                nc.vector.tensor_copy(slot_words[:, lo:hi], words[:].indirect(where))
+                nc.vector.tensor_copy(slot_bytes[:, lo:hi], all_bytes[s][:].indirect(where))
+            x_words.append(slot_words)
+            x_bytes.append(slot_bytes)
+
+        out_sb = []
+        for n in range(N_TILES):
+            window = keep.tile([P, T], F32, name=f"out_sb_{n}")
+            out_sb.append(window)
+
+        sums = {}
+
+        def first_layer(t, s):
+            e = 0 if t == 0 else 1
+            cols = slice(t * P, (t + 1) * P)
+            if s == 0:
+                a = psum_ab.tile([P, H], F32, name="a")
+                b = psum_ab.tile([P, H], F32, name="b")
+                sums[t] = (a, b)
+            for acc, codes, plane in zip(sums[t], (w1, w3), (w1_sc, w3_sc)):
+                nc.tensor.matmul_mx(
+                    out=acc[:],
+                    lhsT=x_words[s][:, cols].bitcast(FP8X4),
+                    lhsT_scale=x_bytes[s][:, cols],
+                    rhs=codes[:, PASSES * e + s, :].bitcast(FP4X4),
+                    rhs_scale=plane[:, PASSES * e + s, :],
+                    start=(s == 0),
+                    stop=(s == PASSES - 1),
+                )
+
+        def second_layer(t):
+            e = 0 if t == 0 else 1
+            a, b = sums[t]
+            act = work.tile([P, H], F32, name="act")
+            nc.scalar.activation(act[:], a[:], ACT.Silu)
+            h = work.tile([P, H], BF16, name="h", align_bytes=64)
+            nc.vector.tensor_tensor(h[:], act[:], b[:], MULT)
+            turned = psum_one.tile([P, 2, P], F32, name="turned")
+            h_pairs = h[:].bitcast(F32)
+            for u in range(2):
+                nc.tensor.transpose(turned[:, u, :], h_pairs[:, u : 2 * P : 2], ident[:])
+            h_grouped = work.tile([P, P, 4], BF16, name="h_grouped", align_bytes=64)
+            nc.scalar.copy(h_grouped[:].bitcast(F32), turned[:].rearrange("p u r -> p r u"))
+            h_words = work.tile([P, P], U32, name="h_words", align_bytes=64)
+            h_bytes = work.tile([P, P], U8, name="h_bytes", align_bytes=64)
+            nc.vector.quantize_mx(
+                out=h_words[:].bitcast(FP8X4), scales=h_bytes[:], in_=h_grouped[:].rearrange("p r j -> p (r j)")
+            )
+            y = psum_one.tile([P, N_TILES, P], F32, name="y")
+            for n in range(N_TILES):
+                nc.tensor.matmul_mx(
+                    out=y[:, n, :],
+                    lhsT=w2[:, e, 2 * P * n : 2 * P * (n + 1)].bitcast(FP4X4),
+                    lhsT_scale=w2_sc[:, e, P * n : P * (n + 1)],
+                    rhs=h_words[:].bitcast(FP8X4),
+                    rhs_scale=h_bytes[:],
+                    start=True,
+                    stop=True,
+                )
+            y_sb = work.tile([P, N_TILES, P], F32, name="y_sb")
+            nc.scalar.copy(y_sb[:], y[:])
+            cols = slice(t * P, (t + 1) * P)
+            where = offsets[:, t * P // 16 : (t + 1) * P // 16]
+            for n in range(N_TILES):
+                nc.vector.tensor_tensor(out_sb[n][:].indirect(where), y_sb[:, n, :], gate_sb[:, cols], MULT)
+
+        for t in range(3):
+            first_layer(t, 0)
+        for t in range(TILES):
+            if t == 3:
+                first_layer(t, 0)
+            first_layer(t, 1)
+            second_layer(t)
+
+        for n in range(N_TILES):
+            nc.sync.dma_start(out[n * P : (n + 1) * P, :], out_sb[n][:])

@@ -20,7 +20,7 @@ MULT = mybir.AluOpType.mult
 
 P = 128
 PASSES = K // 512
-HALF = T // 2
+VECTOR_COLUMNS = (336, 288)
 TILES = T // P
 N_TILES = N // P
 
@@ -34,51 +34,52 @@ def tile_moe_rag_glu_silu_kernel(
     nc = tc.nc
     with ExitStack() as ctx:
         keep = ctx.enter_context(tc.tile_pool(name="keep", bufs=1))
-        work = ctx.enter_context(tc.tile_pool(name="work", bufs=2))
+        work = ctx.enter_context(tc.tile_pool(name="work", bufs=3))
         psum_ab = ctx.enter_context(tc.psum_pool(name="psum_ab", bufs=3))
         psum_one = ctx.enter_context(tc.psum_pool(name="psum_one", bufs=1))
 
         offsets = keep.tile([P, T // 16], U16, name="offsets")
         nc.sync.dma_start(offsets[:], offs)
 
+        def scale_plane(name, scales):
+            plane = keep.tile([P, E * scales.shape[1], scales.shape[3]], U8, name=f"{name}_plane", align_bytes=64)
+            nc.vector.memset(plane[:].bitcast(I32), 0)
+            return plane
+
+        def load_scales(queue, plane, scales):
+            rows = scales.bitcast(I32).rearrange("e s q i -> q (e s) i")
+            for q in range(4):
+                queue.dma_start(plane[32 * q : 32 * q + 4, :, :].bitcast(I32), rows[4 * q : 4 * q + 4, :, :])
+
+        def load_x(s):
+            raw = keep.tile([P, 4, T], F32, name=f"x_raw_{s}")
+            nc.sync.dma_start(raw[:], xT[s * 512 : (s + 1) * 512, :].rearrange("(p j) w -> p j w", j=4))
+            return raw
+
+        def load_words(name, words, s):
+            codes = keep.tile([P, E, words.shape[3]], U8, name=f"{name}_codes_{s}", align_bytes=64)
+            nc.sync.dma_start(codes[:].bitcast(I32), words.bitcast(I32)[:, s, :, :].rearrange("e p b -> p e b"))
+            return codes
+
+        w1_sc = scale_plane("w1", w1_scales)
+        w3_sc = scale_plane("w3", w3_scales)
+        w2_sc = scale_plane("w2", w2_scales)
         all_bytes = []
         for s in range(PASSES):
             plane = keep.tile([P, T], U8, name=f"all_bytes_{s}", align_bytes=64)
-            nc.gpsimd.memset(plane[:], 0)
+            nc.vector.memset(plane[:].bitcast(I32), 0)
             all_bytes.append(plane)
 
-        x_raw = {}
-
-        def load_x(s):
-            rows = xT[s * 512 : (s + 1) * 512, :].rearrange("(p j) w -> p j w", j=4)
-            for half in range(2):
-                raw = keep.tile([P, 4, HALF], F32, name=f"x_raw_{s}_{half}")
-                nc.sync.dma_start(raw[:], rows[:, :, half * HALF : (half + 1) * HALF])
-                x_raw[s, half] = raw
-
-        def load_scales(name, scales):
-            passes, width = scales.shape[1], scales.shape[3]
-            plane = keep.tile([P, E * passes, width], U8, name=f"{name}_plane", align_bytes=64)
-            nc.vector.memset(plane[:].bitcast(I32), 0)
-            rows = scales.bitcast(I32).rearrange("e s q i -> q (e s) i")
-            for q in range(4):
-                nc.sync.dma_start(plane[32 * q : 32 * q + 4, :, :].bitcast(I32), rows[4 * q : 4 * q + 4, :, :])
-            return plane
-
-        def load_words(name, words):
-            passes, width = words.shape[1], words.shape[3]
-            codes = keep.tile([P, E * passes, width], U8, name=f"{name}_codes", align_bytes=64)
-            nc.sync.dma_start(codes[:].bitcast(I32), words.bitcast(I32).rearrange("e s p b -> p (e s) b"))
-            return codes
-
-        load_x(0)
-        w1_sc = load_scales("w1", w1_scales)
-        load_x(1)
-        w3_sc = load_scales("w3", w3_scales)
-        w1 = load_words("w1", w1_words)
-        w3 = load_words("w3", w3_words)
-        w2_sc = load_scales("w2", w2_scales)
-        w2 = load_words("w2", w2_words)
+        x_raw = [load_x(0)]
+        load_scales(nc.sync, w1_sc, w1_scales)
+        load_scales(nc.gpsimd, w3_sc, w3_scales)
+        x_raw.append(load_x(1))
+        w1, w3 = [], []
+        for s in range(PASSES):
+            w1.append(load_words("w1", w1_words, s))
+            w3.append(load_words("w3", w3_words, s))
+        load_scales(nc.gpsimd, w2_sc, w2_scales)
+        w2 = load_words("w2", w2_words, 0)
 
         gate_sb = keep.tile([P, T], F32, name="gate_sb")
         nc.sync.dma_start(gate_sb[:], gate[0:P, :])
@@ -94,19 +95,14 @@ def tile_moe_rag_glu_silu_kernel(
         x_words, x_bytes = [], []
         for s in range(PASSES):
             words = keep.tile([P, T], U32, name=f"all_words_{s}", align_bytes=64)
-            for half in range(2):
-                grouped = keep.tile([P, HALF, 4], BF16, name=f"x_grouped_{s}_{half}", align_bytes=64)
-                src = x_raw[s, half][:].rearrange("p j w -> p w j")
-                if half == 0:
-                    nc.scalar.copy(grouped[:], src)
-                else:
-                    nc.vector.tensor_copy(grouped[:], src)
-                cols = slice(half * HALF, (half + 1) * HALF)
-                nc.vector.quantize_mx(
-                    out=words[:, cols].bitcast(FP8X4),
-                    scales=all_bytes[s][:, cols],
-                    in_=grouped[:].rearrange("p w j -> p (w j)"),
-                )
+            grouped = keep.tile([P, T, 4], BF16, name=f"x_grouped_{s}", align_bytes=64)
+            src = x_raw[s][:].rearrange("p j w -> p w j")
+            cut = VECTOR_COLUMNS[s]
+            nc.vector.tensor_copy(grouped[:, 0:cut, :], src[:, 0:cut, :])
+            nc.scalar.copy(grouped[:, cut:T, :], src[:, cut:T, :])
+            nc.vector.quantize_mx(
+                out=words[:].bitcast(FP8X4), scales=all_bytes[s][:], in_=grouped[:].rearrange("p w j -> p (w j)")
+            )
             slot_words = keep.tile([P, T], U32, name=f"slot_words_{s}", align_bytes=64)
             slot_bytes = keep.tile([P, T], U8, name=f"slot_bytes_{s}", align_bytes=64)
             for e in range(E):
@@ -136,21 +132,26 @@ def tile_moe_rag_glu_silu_kernel(
                     out=acc[:],
                     lhsT=x_words[s][:, cols].bitcast(FP8X4),
                     lhsT_scale=x_bytes[s][:, cols],
-                    rhs=codes[:, PASSES * e + s, :].bitcast(FP4X4),
+                    rhs=codes[s][:, e, :].bitcast(FP4X4),
                     rhs_scale=plane[:, PASSES * e + s, :],
                     start=(s == 0),
                     stop=(s == PASSES - 1),
                 )
 
-        def second_layer(t):
-            e = 0 if t == 0 else 1
+        hidden, results = {}, {}
+
+        def gated(t):
             a, b = sums[t]
             act = work.tile([P, H], F32, name="act")
             nc.scalar.activation(act[:], a[:], ACT.Silu)
             h = work.tile([P, H], BF16, name="h", align_bytes=64)
             nc.vector.tensor_tensor(h[:], act[:], b[:], MULT)
+            hidden[t] = h
+
+        def second_layer(t):
+            e = 0 if t == 0 else 1
             turned = psum_one.tile([P, 2, P], F32, name="turned")
-            h_pairs = h[:].bitcast(F32)
+            h_pairs = hidden[t][:].bitcast(F32)
             for u in range(2):
                 nc.tensor.transpose(turned[:, u, :], h_pairs[:, u : 2 * P : 2], ident[:])
             h_grouped = work.tile([P, P, 4], BF16, name="h_grouped", align_bytes=64)
@@ -173,18 +174,33 @@ def tile_moe_rag_glu_silu_kernel(
                 )
             y_sb = work.tile([P, N_TILES, P], F32, name="y_sb")
             nc.scalar.copy(y_sb[:], y[:])
+            results[t] = y_sb
+
+        def scatter(t):
             cols = slice(t * P, (t + 1) * P)
             where = offsets[:, t * P // 16 : (t + 1) * P // 16]
             for n in range(N_TILES):
-                nc.vector.tensor_tensor(out_sb[n][:].indirect(where), y_sb[:, n, :], gate_sb[:, cols], MULT)
+                nc.vector.tensor_tensor(out_sb[n][:].indirect(where), results[t][:, n, :], gate_sb[:, cols], MULT)
 
         for t in range(3):
             first_layer(t, 0)
-        for t in range(TILES):
-            if t == 3:
-                first_layer(t, 0)
-            first_layer(t, 1)
-            second_layer(t)
+        first_layer(0, 1)
+        gated(0)
+        first_layer(1, 1)
+        gated(1)
+        second_layer(0)
+        first_layer(2, 1)
+        gated(2)
+        second_layer(1)
+        scatter(0)
+        first_layer(3, 0)
+        first_layer(3, 1)
+        gated(3)
+        second_layer(2)
+        scatter(1)
+        second_layer(3)
+        scatter(2)
+        scatter(3)
 
         for n in range(N_TILES):
             nc.sync.dma_start(out[n * P : (n + 1) * P, :], out_sb[n][:])

@@ -20,9 +20,12 @@ MULT = mybir.AluOpType.mult
 
 P = 128
 PASSES = K // 512
-VECTOR_COLUMNS = (336, 288)
+HALF = T // 2
+VECTOR_COLUMNS = ((160, 160), (96, 128))
 TILES = T // P
 N_TILES = N // P
+GROUPS = ((0, 128), (128, 384), (384, 512))
+GROUP_OF = (0, 1, 1, 2)
 
 FLOPS = 2 * T * (2 * K * H + H * N)
 BYTES = 4 * K * T + 2 * E * (K * H // 2 + K * H // 32) + E * (H * N // 2 + H * N // 32) + 4 * P * T + 2 * P * (T // 16) + 4 * N * T
@@ -52,13 +55,17 @@ def tile_moe_rag_glu_silu_kernel(
                 queue.dma_start(plane[32 * q : 32 * q + 4, :, :].bitcast(I32), rows[4 * q : 4 * q + 4, :, :])
 
         def load_x(s):
-            raw = keep.tile([P, 4, T], F32, name=f"x_raw_{s}")
-            nc.sync.dma_start(raw[:], xT[s * 512 : (s + 1) * 512, :].rearrange("(p j) w -> p j w", j=4))
-            return raw
+            rows = xT[s * 512 : (s + 1) * 512, :].rearrange("(p j) w -> p j w", j=4)
+            halves = []
+            for half in range(2):
+                raw = keep.tile([P, 4, HALF], F32, name=f"x_raw_{s}_{half}")
+                nc.sync.dma_start(raw[:], rows[:, :, half * HALF : (half + 1) * HALF])
+                halves.append(raw)
+            return halves
 
-        def load_words(name, words, s):
-            codes = keep.tile([P, E, words.shape[3]], U8, name=f"{name}_codes_{s}", align_bytes=64)
-            nc.sync.dma_start(codes[:].bitcast(I32), words.bitcast(I32)[:, s, :, :].rearrange("e p b -> p e b"))
+        def load_words(name, words, e):
+            codes = keep.tile([P, words.shape[1], words.shape[3]], U8, name=f"{name}_codes_{e}", align_bytes=64)
+            nc.sync.dma_start(codes[:].bitcast(I32), words.bitcast(I32)[e].rearrange("s p b -> p s b"))
             return codes
 
         w1_sc = scale_plane("w1", w1_scales)
@@ -72,14 +79,15 @@ def tile_moe_rag_glu_silu_kernel(
 
         x_raw = [load_x(0)]
         load_scales(nc.sync, w1_sc, w1_scales)
-        load_scales(nc.gpsimd, w3_sc, w3_scales)
         x_raw.append(load_x(1))
+        load_scales(nc.sync, w3_sc, w3_scales)
         w1, w3 = [], []
-        for s in range(PASSES):
-            w1.append(load_words("w1", w1_words, s))
-            w3.append(load_words("w3", w3_words, s))
-        load_scales(nc.gpsimd, w2_sc, w2_scales)
-        w2 = load_words("w2", w2_words, 0)
+        for e in range(E):
+            w1.append(load_words("w1", w1_words, e))
+            w3.append(load_words("w3", w3_words, e))
+        load_scales(nc.sync, w2_sc, w2_scales)
+        w2 = keep.tile([P, E, 2 * N], U8, name="w2", align_bytes=64)
+        nc.sync.dma_start(w2[:].bitcast(I32), w2_words.bitcast(I32)[:, 0].rearrange("e p b -> p e b"))
 
         gate_sb = keep.tile([P, T], F32, name="gate_sb")
         nc.sync.dma_start(gate_sb[:], gate[0:P, :])
@@ -95,14 +103,18 @@ def tile_moe_rag_glu_silu_kernel(
         x_words, x_bytes = [], []
         for s in range(PASSES):
             words = keep.tile([P, T], U32, name=f"all_words_{s}", align_bytes=64)
-            grouped = keep.tile([P, T, 4], BF16, name=f"x_grouped_{s}", align_bytes=64)
-            src = x_raw[s][:].rearrange("p j w -> p w j")
-            cut = VECTOR_COLUMNS[s]
-            nc.vector.tensor_copy(grouped[:, 0:cut, :], src[:, 0:cut, :])
-            nc.scalar.copy(grouped[:, cut:T, :], src[:, cut:T, :])
-            nc.vector.quantize_mx(
-                out=words[:].bitcast(FP8X4), scales=all_bytes[s][:], in_=grouped[:].rearrange("p w j -> p (w j)")
-            )
+            for half in range(2):
+                grouped = keep.tile([P, HALF, 4], BF16, name=f"x_grouped_{s}_{half}", align_bytes=64)
+                src = x_raw[s][half][:].rearrange("p j w -> p w j")
+                cut = VECTOR_COLUMNS[s][half]
+                nc.scalar.copy(grouped[:, cut:HALF, :], src[:, cut:HALF, :])
+                nc.vector.tensor_copy(grouped[:, 0:cut, :], src[:, 0:cut, :])
+                cols = slice(half * HALF, (half + 1) * HALF)
+                nc.vector.quantize_mx(
+                    out=words[:, cols].bitcast(FP8X4),
+                    scales=all_bytes[s][:, cols],
+                    in_=grouped[:].rearrange("p w j -> p (w j)"),
+                )
             slot_words = keep.tile([P, T], U32, name=f"slot_words_{s}", align_bytes=64)
             slot_bytes = keep.tile([P, T], U8, name=f"slot_bytes_{s}", align_bytes=64)
             for e in range(E):
@@ -132,7 +144,7 @@ def tile_moe_rag_glu_silu_kernel(
                     out=acc[:],
                     lhsT=x_words[s][:, cols].bitcast(FP8X4),
                     lhsT_scale=x_bytes[s][:, cols],
-                    rhs=codes[s][:, e, :].bitcast(FP4X4),
+                    rhs=codes[e][:, s, :].bitcast(FP4X4),
                     rhs_scale=plane[:, PASSES * e + s, :],
                     start=(s == 0),
                     stop=(s == PASSES - 1),
@@ -172,15 +184,18 @@ def tile_moe_rag_glu_silu_kernel(
                     start=True,
                     stop=True,
                 )
-            y_sb = work.tile([P, N_TILES, P], F32, name="y_sb")
-            nc.scalar.copy(y_sb[:], y[:])
-            results[t] = y_sb
+            group = GROUP_OF[t]
+            lo, hi = GROUPS[group]
+            if lo == t * P:
+                y_sb = keep.tile([P, N_TILES, hi - lo], F32, name=f"y_sb_{group}")
+                results[group] = y_sb
+            nc.scalar.copy(results[group][:, :, t * P - lo : (t + 1) * P - lo], y[:])
 
-        def scatter(t):
-            cols = slice(t * P, (t + 1) * P)
-            where = offsets[:, t * P // 16 : (t + 1) * P // 16]
+        def scatter(group):
+            lo, hi = GROUPS[group]
+            where = offsets[:, lo // 16 : hi // 16]
             for n in range(N_TILES):
-                nc.vector.tensor_tensor(out_sb[n][:].indirect(where), results[t][:, n, :], gate_sb[:, cols], MULT)
+                nc.vector.tensor_tensor(out_sb[n][:].indirect(where), results[group][:, n, :], gate_sb[:, lo:hi], MULT)
 
         for t in range(3):
             first_layer(t, 0)
@@ -192,15 +207,14 @@ def tile_moe_rag_glu_silu_kernel(
         first_layer(2, 1)
         gated(2)
         second_layer(1)
-        scatter(0)
         first_layer(3, 0)
         first_layer(3, 1)
         gated(3)
         second_layer(2)
-        scatter(1)
+        scatter(0)
         second_layer(3)
+        scatter(1)
         scatter(2)
-        scatter(3)
 
         for n in range(N_TILES):
             nc.sync.dma_start(out[n * P : (n + 1) * P, :], out_sb[n][:])

@@ -4,8 +4,6 @@ import concourse.mybir as mybir
 from concourse.masks import make_identity
 
 K, T, E, H, N = 1024, 512, 2, 512, 384
-COUNTS = (128, 384)
-STARTS = (0, 128)
 
 F32 = mybir.dt.float32
 BF16 = mybir.dt.bfloat16
@@ -21,11 +19,10 @@ MULT = mybir.AluOpType.mult
 P = 128
 PASSES = K // 512
 HALF = T // 2
-VECTOR_COLUMNS = ((160, 160), (96, 128))
+VECTOR_COLUMNS = ((160, 160), (0, 128))
 TILES = T // P
 N_TILES = N // P
 GROUPS = ((0, 128), (128, 384), (384, 512))
-GROUP_OF = (0, 1, 1, 2)
 
 FLOPS = 2 * T * (2 * K * H + H * N)
 BYTES = 4 * K * T + 2 * E * (K * H // 2 + K * H // 32) + E * (H * N // 2 + H * N // 32) + 4 * P * T + 2 * P * (T // 16) + 4 * N * T
@@ -42,7 +39,6 @@ def tile_moe_rag_glu_silu_kernel(
         psum_one = ctx.enter_context(tc.psum_pool(name="psum_one", bufs=1))
 
         offsets = keep.tile([P, T // 16], U16, name="offsets")
-        nc.sync.dma_start(offsets[:], offs)
 
         def scale_plane(name, scales):
             plane = keep.tile([P, E * scales.shape[1], scales.shape[3]], U8, name=f"{name}_plane", align_bytes=64)
@@ -78,6 +74,7 @@ def tile_moe_rag_glu_silu_kernel(
             all_bytes.append(plane)
 
         x_raw = [load_x(0)]
+        nc.sync.dma_start(offsets[:], offs)
         load_scales(nc.sync, w1_sc, w1_scales)
         x_raw.append(load_x(1))
         load_scales(nc.sync, w3_sc, w3_scales)
@@ -100,37 +97,48 @@ def tile_moe_rag_glu_silu_kernel(
         warm_out = keep.tile([P, 1], F32, name="warm_out")
         nc.scalar.activation(warm_out[:], warm[:], ACT.Silu)
 
-        x_words, x_bytes = [], []
+        grouped, all_words, x_words, x_bytes = {}, [], [], []
         for s in range(PASSES):
             words = keep.tile([P, T], U32, name=f"all_words_{s}", align_bytes=64)
-            for half in range(2):
-                grouped = keep.tile([P, HALF, 4], BF16, name=f"x_grouped_{s}_{half}", align_bytes=64)
-                src = x_raw[s][half][:].rearrange("p j w -> p w j")
-                cut = VECTOR_COLUMNS[s][half]
-                nc.scalar.copy(grouped[:, cut:HALF, :], src[:, cut:HALF, :])
-                nc.vector.tensor_copy(grouped[:, 0:cut, :], src[:, 0:cut, :])
-                cols = slice(half * HALF, (half + 1) * HALF)
-                nc.vector.quantize_mx(
-                    out=words[:, cols].bitcast(FP8X4),
-                    scales=all_bytes[s][:, cols],
-                    in_=grouped[:].rearrange("p w j -> p (w j)"),
-                )
             slot_words = keep.tile([P, T], U32, name=f"slot_words_{s}", align_bytes=64)
             slot_bytes = keep.tile([P, T], U8, name=f"slot_bytes_{s}", align_bytes=64)
-            for e in range(E):
-                lo, hi = STARTS[e], STARTS[e] + COUNTS[e]
-                where = offsets[:, lo // 16 : hi // 16]
-                nc.vector.tensor_copy(slot_words[:, lo:hi], words[:].indirect(where))
-                nc.vector.tensor_copy(slot_bytes[:, lo:hi], all_bytes[s][:].indirect(where))
+            all_words.append(words)
             x_words.append(slot_words)
             x_bytes.append(slot_bytes)
-
+            for half in range(2):
+                tokens = keep.tile([P, HALF, 4], BF16, name=f"grouped_{s}_{half}", align_bytes=64)
+                grouped[s, half] = tokens
         out_sb = []
         for n in range(N_TILES):
             window = keep.tile([P, T], F32, name=f"out_sb_{n}")
             out_sb.append(window)
+        sums, acts, hidden, turned, h_grouped, h_codes, y_sums, y_sb = {}, {}, {}, {}, {}, {}, {}, {}
 
-        sums = {}
+        def cast(engine_copy, s, half, lo, hi):
+            engine_copy(
+                grouped[s, half][:, lo:hi, :].rearrange("p (c i) j -> p c j i", i=4),
+                x_raw[s][half][:, :, lo:hi].rearrange("p j (c i) -> p c j i", i=4),
+            )
+
+        def cast_s(s, half):
+            cast(nc.scalar.copy, s, half, VECTOR_COLUMNS[s][half], HALF)
+
+        def cast_v(s, half):
+            cast(nc.vector.tensor_copy, s, half, 0, VECTOR_COLUMNS[s][half])
+
+        def quantise_x(s, half):
+            cols = slice(half * HALF, (half + 1) * HALF)
+            nc.vector.quantize_mx(
+                out=all_words[s][:, cols].bitcast(FP8X4),
+                scales=all_bytes[s][:, cols],
+                in_=grouped[s, half][:].rearrange("p w j -> p (w j)"),
+            )
+
+        def gather(s, group):
+            lo, hi = GROUPS[group]
+            where = offsets[:, lo // 16 : hi // 16]
+            nc.vector.tensor_copy(x_words[s][:, lo:hi], all_words[s][:].indirect(where))
+            nc.vector.tensor_copy(x_bytes[s][:, lo:hi], all_bytes[s][:].indirect(where))
 
         def first_layer(t, s):
             e = 0 if t == 0 else 1
@@ -150,29 +158,39 @@ def tile_moe_rag_glu_silu_kernel(
                     stop=(s == PASSES - 1),
                 )
 
-        hidden, results = {}, {}
-
-        def gated(t):
-            a, b = sums[t]
+        def silu(t):
             act = work.tile([P, H], F32, name="act")
-            nc.scalar.activation(act[:], a[:], ACT.Silu)
+            nc.scalar.activation(act[:], sums[t][0][:], ACT.Silu)
+            acts[t] = act
+
+        def multiply(t):
             h = work.tile([P, H], BF16, name="h", align_bytes=64)
-            nc.vector.tensor_tensor(h[:], act[:], b[:], MULT)
+            nc.vector.tensor_tensor(h[:], acts[t][:], sums[t][1][:], MULT)
             hidden[t] = h
 
-        def second_layer(t):
-            e = 0 if t == 0 else 1
-            turned = psum_one.tile([P, 2, P], F32, name="turned")
-            h_pairs = hidden[t][:].bitcast(F32)
+        def turn(t):
+            bank = psum_one.tile([P, 2, P], F32, name="turned")
+            pairs = hidden[t][:].bitcast(F32)
             for u in range(2):
-                nc.tensor.transpose(turned[:, u, :], h_pairs[:, u : 2 * P : 2], ident[:])
-            h_grouped = work.tile([P, P, 4], BF16, name="h_grouped", align_bytes=64)
-            nc.scalar.copy(h_grouped[:].bitcast(F32), turned[:].rearrange("p u r -> p r u"))
+                nc.tensor.transpose(bank[:, u, :], pairs[:, u : 2 * P : 2], ident[:])
+            turned[t] = bank
+
+        def group_h(t):
+            h4 = work.tile([P, P, 4], BF16, name="h4", align_bytes=64)
+            nc.scalar.copy(h4[:].bitcast(F32), turned[t][:].rearrange("p u r -> p r u"))
+            h_grouped[t] = h4
+
+        def quantise_h(t):
             h_words = work.tile([P, P], U32, name="h_words", align_bytes=64)
             h_bytes = work.tile([P, P], U8, name="h_bytes", align_bytes=64)
             nc.vector.quantize_mx(
-                out=h_words[:].bitcast(FP8X4), scales=h_bytes[:], in_=h_grouped[:].rearrange("p r j -> p (r j)")
+                out=h_words[:].bitcast(FP8X4), scales=h_bytes[:], in_=h_grouped[t][:].rearrange("p r j -> p (r j)")
             )
+            h_codes[t] = (h_words, h_bytes)
+
+        def second_layer(t):
+            e = 0 if t == 0 else 1
+            h_words, h_bytes = h_codes[t]
             y = psum_one.tile([P, N_TILES, P], F32, name="y")
             for n in range(N_TILES):
                 nc.tensor.matmul_mx(
@@ -184,37 +202,76 @@ def tile_moe_rag_glu_silu_kernel(
                     start=True,
                     stop=True,
                 )
-            group = GROUP_OF[t]
-            lo, hi = GROUPS[group]
-            if lo == t * P:
-                y_sb = keep.tile([P, N_TILES, hi - lo], F32, name=f"y_sb_{group}")
-                results[group] = y_sb
-            nc.scalar.copy(results[group][:, :, t * P - lo : (t + 1) * P - lo], y[:])
+            y_sums[t] = y
 
-        def scatter(group):
-            lo, hi = GROUPS[group]
-            where = offsets[:, lo // 16 : hi // 16]
+        def empty_y(t):
+            result = work.tile([P, N_TILES, P], F32, name="result")
+            nc.scalar.copy(result[:], y_sums[t][:])
+            y_sb[t] = result
+
+        def scatter(t):
+            cols = slice(t * P, (t + 1) * P)
+            where = offsets[:, t * P // 16 : (t + 1) * P // 16]
             for n in range(N_TILES):
-                nc.vector.tensor_tensor(out_sb[n][:].indirect(where), results[group][:, n, :], gate_sb[:, lo:hi], MULT)
+                nc.vector.tensor_tensor(out_sb[n][:].indirect(where), y_sb[t][:, n, :], gate_sb[:, cols], MULT)
 
-        for t in range(3):
-            first_layer(t, 0)
+        cast_s(0, 0)
+        cast_v(0, 0)
+        quantise_x(0, 0)
+        cast_s(0, 1)
+        cast_v(0, 1)
+        quantise_x(0, 1)
+        gather(0, 0)
+        gather(0, 1)
+        cast_s(1, 0)
+        cast_s(1, 1)
+        quantise_x(1, 0)
+        cast_v(1, 1)
+        quantise_x(1, 1)
+        gather(1, 0)
+        first_layer(0, 0)
         first_layer(0, 1)
-        gated(0)
+        first_layer(1, 0)
+        gather(1, 1)
+        silu(0)
         first_layer(1, 1)
-        gated(1)
-        second_layer(0)
+        gather(0, 2)
+        multiply(0)
+        turn(0)
+        silu(1)
+        first_layer(2, 0)
+        group_h(0)
+        gather(1, 2)
+        multiply(1)
         first_layer(2, 1)
-        gated(2)
-        second_layer(1)
+        quantise_h(0)
+        silu(2)
+        turn(1)
+        second_layer(0)
+        multiply(2)
+        group_h(1)
+        quantise_h(1)
+        empty_y(0)
         first_layer(3, 0)
-        first_layer(3, 1)
-        gated(3)
-        second_layer(2)
         scatter(0)
-        second_layer(3)
+        first_layer(3, 1)
+        silu(3)
+        turn(2)
+        multiply(3)
+        second_layer(1)
+        empty_y(1)
+        group_h(2)
+        turn(3)
+        quantise_h(2)
+        second_layer(2)
+        group_h(3)
         scatter(1)
+        quantise_h(3)
+        empty_y(2)
+        second_layer(3)
         scatter(2)
+        empty_y(3)
+        scatter(3)
 
         for n in range(N_TILES):
             nc.sync.dma_start(out[n * P : (n + 1) * P, :], out_sb[n][:])

@@ -19,7 +19,7 @@ MULT = mybir.AluOpType.mult
 P = 128
 PASSES = K // 512
 HALF = T // 2
-VECTOR_COLUMNS = ((160, 160), (0, 128))
+VECTOR_COLUMNS = ((192, 192), (0, 160))
 TILES = T // P
 N_TILES = N // P
 GROUPS = ((0, 128), (128, 384), (384, 512))
@@ -134,11 +134,15 @@ def tile_moe_rag_glu_silu_kernel(
                 in_=grouped[s, half][:].rearrange("p w j -> p (w j)"),
             )
 
-        def gather(s, group):
+        def gather(picked, tokens, group):
             lo, hi = GROUPS[group]
-            where = offsets[:, lo // 16 : hi // 16]
-            nc.vector.tensor_copy(x_words[s][:, lo:hi], all_words[s][:].indirect(where))
-            nc.vector.tensor_copy(x_bytes[s][:, lo:hi], all_bytes[s][:].indirect(where))
+            nc.vector.tensor_copy(picked[:, lo:hi], tokens[:].indirect(offsets[:, lo // 16 : hi // 16]))
+
+        def gather_words(s, group):
+            gather(x_words[s], all_words[s], group)
+
+        def gather_bytes(s, group):
+            gather(x_bytes[s], all_bytes[s], group)
 
         def first_layer(t, s):
             e = 0 if t == 0 else 1
@@ -164,15 +168,20 @@ def tile_moe_rag_glu_silu_kernel(
             acts[t] = act
 
         def multiply(t):
-            h = work.tile([P, H], BF16, name="h", align_bytes=64)
-            nc.vector.tensor_tensor(h[:], acts[t][:], sums[t][1][:], MULT)
+            h = work.tile([P, 2, P, 2], BF16, name="h", align_bytes=64)
+            nc.vector.tensor_tensor(
+                h[:],
+                acts[t][:].rearrange("p (q u d) -> p u q d", u=2, d=2),
+                sums[t][1][:].rearrange("p (q u d) -> p u q d", u=2, d=2),
+                MULT,
+            )
             hidden[t] = h
 
         def turn(t):
             bank = psum_one.tile([P, 2, P], F32, name="turned")
-            pairs = hidden[t][:].bitcast(F32)
+            pairs = hidden[t][:].rearrange("p u q d -> p (u q d)").bitcast(F32)
             for u in range(2):
-                nc.tensor.transpose(bank[:, u, :], pairs[:, u : 2 * P : 2], ident[:])
+                nc.tensor.transpose(bank[:, u, :], pairs[:, u * P : (u + 1) * P], ident[:])
             turned[t] = bank
 
         def group_h(t):
@@ -209,69 +218,82 @@ def tile_moe_rag_glu_silu_kernel(
             nc.scalar.copy(result[:], y_sums[t][:])
             y_sb[t] = result
 
-        def scatter(t):
+        def scatter(t, n):
             cols = slice(t * P, (t + 1) * P)
             where = offsets[:, t * P // 16 : (t + 1) * P // 16]
-            for n in range(N_TILES):
-                nc.vector.tensor_tensor(out_sb[n][:].indirect(where), y_sb[t][:, n, :], gate_sb[:, cols], MULT)
+            nc.vector.tensor_tensor(out_sb[n][:].indirect(where), y_sb[t][:, n, :], gate_sb[:, cols], MULT)
 
         cast_s(0, 0)
         cast_v(0, 0)
         quantise_x(0, 0)
         cast_s(0, 1)
         cast_v(0, 1)
-        quantise_x(0, 1)
-        gather(0, 0)
-        gather(0, 1)
         cast_s(1, 0)
+        quantise_x(0, 1)
+        gather_words(0, 0)
+        gather_words(0, 1)
         cast_s(1, 1)
-        quantise_x(1, 0)
+        gather_bytes(0, 0)
         cast_v(1, 1)
+        quantise_x(1, 0)
         quantise_x(1, 1)
-        gather(1, 0)
+        gather_bytes(0, 1)
+        gather_words(1, 0)
+        gather_bytes(1, 0)
         first_layer(0, 0)
+        gather_bytes(1, 1)
         first_layer(0, 1)
-        first_layer(1, 0)
-        gather(1, 1)
         silu(0)
+        first_layer(1, 0)
+        gather_words(1, 1)
         first_layer(1, 1)
-        gather(0, 2)
-        multiply(0)
-        turn(0)
         silu(1)
         first_layer(2, 0)
-        group_h(0)
-        gather(1, 2)
+        gather_words(0, 2)
+        multiply(0)
+        gather_bytes(1, 2)
+        gather_bytes(0, 2)
         multiply(1)
+        turn(0)
         first_layer(2, 1)
-        quantise_h(0)
-        silu(2)
-        turn(1)
-        second_layer(0)
-        multiply(2)
-        group_h(1)
-        quantise_h(1)
-        empty_y(0)
+        group_h(0)
         first_layer(3, 0)
-        scatter(0)
+        quantise_h(0)
+        turn(1)
+        silu(2)
+        second_layer(0)
+        gather_words(1, 2)
         first_layer(3, 1)
+        group_h(1)
+        empty_y(0)
+        multiply(2)
+        quantise_h(1)
+        scatter(0, 0)
         silu(3)
         turn(2)
+        group_h(2)
         multiply(3)
         second_layer(1)
-        empty_y(1)
-        group_h(2)
-        turn(3)
         quantise_h(2)
-        second_layer(2)
+        empty_y(1)
+        scatter(0, 1)
+        turn(3)
         group_h(3)
-        scatter(1)
+        scatter(1, 0)
+        scatter(1, 1)
         quantise_h(3)
+        second_layer(2)
+        scatter(0, 2)
         empty_y(2)
+        scatter(1, 2)
         second_layer(3)
-        scatter(2)
         empty_y(3)
-        scatter(3)
+        scatter(2, 0)
+        scatter(2, 1)
+        scatter(2, 2)
+        scatter(3, 0)
+        scatter(3, 1)
+        scatter(3, 2)
 
         for n in range(N_TILES):
             nc.sync.dma_start(out[n * P : (n + 1) * P, :], out_sb[n][:])

from contextlib import ExitStack

import concourse.mybir as mybir
from concourse.masks import make_identity

K, T, E, H, N = 1024, 512, 2, 512, 384

F32 = mybir.dt.float32
BF16 = mybir.dt.bfloat16
I32 = mybir.dt.int32
U32 = mybir.dt.uint32
U16 = mybir.dt.uint16
U8 = mybir.dt.uint8
FP8X4 = mybir.dt.float8_e4m3fn_x4
FP4X4 = mybir.dt.float4_e2m1fn_x4
ACT = mybir.ActivationFunctionType
MULT = mybir.AluOpType.mult

P = 128
PASSES = K // 512
HALF = T // 2
VECTOR_COLUMNS = ((192, 192), (0, 160))
TILES = T // P
N_TILES = N // P
GROUPS = ((0, 128), (128, 384), (384, 512))

FLOPS = 2 * T * (2 * K * H + H * N)
BYTES = 4 * K * T + 2 * E * (K * H // 2 + K * H // 32) + E * (H * N // 2 + H * N // 32) + 4 * P * T + 2 * P * (T // 16) + 4 * N * T


def tile_moe_rag_glu_silu_kernel(
    tc, xT, w1_words, w1_scales, w3_words, w3_scales, w2_words, w2_scales, gate, offs, out
):
    nc = tc.nc
    with ExitStack() as ctx:
        keep = ctx.enter_context(tc.tile_pool(name="keep", bufs=1))
        work = ctx.enter_context(tc.tile_pool(name="work", bufs=3))
        psum_ab = ctx.enter_context(tc.psum_pool(name="psum_ab", bufs=3))
        psum_one = ctx.enter_context(tc.psum_pool(name="psum_one", bufs=1))

        offsets = keep.tile([P, T // 16], U16, name="offsets")

        def scale_plane(name, scales):
            plane = keep.tile([P, E * scales.shape[1], scales.shape[3]], U8, name=f"{name}_plane", align_bytes=64)
            nc.vector.memset(plane[:].bitcast(I32), 0)
            return plane

        def load_scales(queue, plane, scales):
            rows = scales.bitcast(I32).rearrange("e s q i -> q (e s) i")
            for q in range(4):
                queue.dma_start(plane[32 * q : 32 * q + 4, :, :].bitcast(I32), rows[4 * q : 4 * q + 4, :, :])

        def load_x(s):
            rows = xT[s * 512 : (s + 1) * 512, :].rearrange("(p j) w -> p j w", j=4)
            halves = []
            for half in range(2):
                raw = keep.tile([P, 4, HALF], F32, name=f"x_raw_{s}_{half}")
                nc.sync.dma_start(raw[:], rows[:, :, half * HALF : (half + 1) * HALF])
                halves.append(raw)
            return halves

        def load_words(name, words, e):
            codes = keep.tile([P, words.shape[1], words.shape[3]], U8, name=f"{name}_codes_{e}", align_bytes=64)
            nc.sync.dma_start(codes[:].bitcast(I32), words.bitcast(I32)[e].rearrange("s p b -> p s b"))
            return codes

        w1_sc = scale_plane("w1", w1_scales)
        w3_sc = scale_plane("w3", w3_scales)
        w2_sc = scale_plane("w2", w2_scales)
        all_bytes = []
        for s in range(PASSES):
            plane = keep.tile([P, T], U8, name=f"all_bytes_{s}", align_bytes=64)
            nc.vector.memset(plane[:].bitcast(I32), 0)
            all_bytes.append(plane)

        x_raw = [load_x(0)]
        nc.sync.dma_start(offsets[:], offs)
        load_scales(nc.sync, w1_sc, w1_scales)
        x_raw.append(load_x(1))
        load_scales(nc.sync, w3_sc, w3_scales)
        w1, w3 = [], []
        for e in range(E):
            w1.append(load_words("w1", w1_words, e))
            w3.append(load_words("w3", w3_words, e))
        load_scales(nc.sync, w2_sc, w2_scales)
        w2 = keep.tile([P, E, 2 * N], U8, name="w2", align_bytes=64)
        nc.sync.dma_start(w2[:].bitcast(I32), w2_words.bitcast(I32)[:, 0].rearrange("e p b -> p e b"))

        gate_sb = keep.tile([P, T], F32, name="gate_sb")
        nc.sync.dma_start(gate_sb[:], gate[0:P, :])

        ident = keep.tile([P, P], F32, name="ident")
        make_identity(nc, ident[:])

        warm = keep.tile([P, 1], F32, name="warm")
        nc.vector.memset(warm[:], 0.0)
        warm_out = keep.tile([P, 1], F32, name="warm_out")
        nc.scalar.activation(warm_out[:], warm[:], ACT.Silu)

        grouped, all_words, x_words, x_bytes = {}, [], [], []
        for s in range(PASSES):
            words = keep.tile([P, T], U32, name=f"all_words_{s}", align_bytes=64)
            slot_words = keep.tile([P, T], U32, name=f"slot_words_{s}", align_bytes=64)
            slot_bytes = keep.tile([P, T], U8, name=f"slot_bytes_{s}", align_bytes=64)
            all_words.append(words)
            x_words.append(slot_words)
            x_bytes.append(slot_bytes)
            for half in range(2):
                tokens = keep.tile([P, HALF, 4], BF16, name=f"grouped_{s}_{half}", align_bytes=64)
                grouped[s, half] = tokens
        out_sb = []
        for n in range(N_TILES):
            window = keep.tile([P, T], F32, name=f"out_sb_{n}")
            out_sb.append(window)
        sums, acts, hidden, turned, h_grouped, h_codes, y_sums, y_sb = {}, {}, {}, {}, {}, {}, {}, {}

        def cast(engine_copy, s, half, lo, hi):
            engine_copy(
                grouped[s, half][:, lo:hi, :].rearrange("p (c i) j -> p c j i", i=4),
                x_raw[s][half][:, :, lo:hi].rearrange("p j (c i) -> p c j i", i=4),
            )

        def cast_s(s, half):
            cast(nc.scalar.copy, s, half, VECTOR_COLUMNS[s][half], HALF)

        def cast_v(s, half):
            cast(nc.vector.tensor_copy, s, half, 0, VECTOR_COLUMNS[s][half])

        def quantise_x(s, half):
            cols = slice(half * HALF, (half + 1) * HALF)
            nc.vector.quantize_mx(
                out=all_words[s][:, cols].bitcast(FP8X4),
                scales=all_bytes[s][:, cols],
                in_=grouped[s, half][:].rearrange("p w j -> p (w j)"),
            )

        def gather(picked, tokens, group):
            lo, hi = GROUPS[group]
            nc.vector.tensor_copy(picked[:, lo:hi], tokens[:].indirect(offsets[:, lo // 16 : hi // 16]))

        def gather_words(s, group):
            gather(x_words[s], all_words[s], group)

        def gather_bytes(s, group):
            gather(x_bytes[s], all_bytes[s], group)

        def first_layer(t, s):
            e = 0 if t == 0 else 1
            cols = slice(t * P, (t + 1) * P)
            if s == 0:
                a = psum_ab.tile([P, H], F32, name="a")
                b = psum_ab.tile([P, H], F32, name="b")
                sums[t] = (a, b)
            for acc, codes, plane in zip(sums[t], (w1, w3), (w1_sc, w3_sc)):
                nc.tensor.matmul_mx(
                    out=acc[:],
                    lhsT=x_words[s][:, cols].bitcast(FP8X4),
                    lhsT_scale=x_bytes[s][:, cols],
                    rhs=codes[e][:, s, :].bitcast(FP4X4),
                    rhs_scale=plane[:, PASSES * e + s, :],
                    start=(s == 0),
                    stop=(s == PASSES - 1),
                )

        def silu(t):
            act = work.tile([P, H], F32, name="act")
            nc.scalar.activation(act[:], sums[t][0][:], ACT.Silu)
            acts[t] = act

        def multiply(t):
            h = work.tile([P, 2, P, 2], BF16, name="h", align_bytes=64)
            nc.vector.tensor_tensor(
                h[:],
                acts[t][:].rearrange("p (q u d) -> p u q d", u=2, d=2),
                sums[t][1][:].rearrange("p (q u d) -> p u q d", u=2, d=2),
                MULT,
            )
            hidden[t] = h

        def turn(t):
            bank = psum_one.tile([P, 2, P], F32, name="turned")
            pairs = hidden[t][:].rearrange("p u q d -> p (u q d)").bitcast(F32)
            for u in range(2):
                nc.tensor.transpose(bank[:, u, :], pairs[:, u * P : (u + 1) * P], ident[:])
            turned[t] = bank

        def group_h(t):
            h4 = work.tile([P, P, 4], BF16, name="h4", align_bytes=64)
            nc.scalar.copy(h4[:].bitcast(F32), turned[t][:].rearrange("p u r -> p r u"))
            h_grouped[t] = h4

        def quantise_h(t):
            h_words = work.tile([P, P], U32, name="h_words", align_bytes=64)
            h_bytes = work.tile([P, P], U8, name="h_bytes", align_bytes=64)
            nc.vector.quantize_mx(
                out=h_words[:].bitcast(FP8X4), scales=h_bytes[:], in_=h_grouped[t][:].rearrange("p r j -> p (r j)")
            )
            h_codes[t] = (h_words, h_bytes)

        def second_layer(t):
            e = 0 if t == 0 else 1
            h_words, h_bytes = h_codes[t]
            y = psum_one.tile([P, N_TILES, P], F32, name="y")
            for n in range(N_TILES):
                nc.tensor.matmul_mx(
                    out=y[:, n, :],
                    lhsT=w2[:, e, 2 * P * n : 2 * P * (n + 1)].bitcast(FP4X4),
                    lhsT_scale=w2_sc[:, e, P * n : P * (n + 1)],
                    rhs=h_words[:].bitcast(FP8X4),
                    rhs_scale=h_bytes[:],
                    start=True,
                    stop=True,
                )
            y_sums[t] = y

        def empty_y(t):
            result = work.tile([P, N_TILES, P], F32, name="result")
            nc.scalar.copy(result[:], y_sums[t][:])
            y_sb[t] = result

        def scatter(t, n):
            cols = slice(t * P, (t + 1) * P)
            where = offsets[:, t * P // 16 : (t + 1) * P // 16]
            nc.vector.tensor_tensor(out_sb[n][:].indirect(where), y_sb[t][:, n, :], gate_sb[:, cols], MULT)

        cast_s(0, 0)
        cast_v(0, 0)
        quantise_x(0, 0)
        cast_s(0, 1)
        cast_v(0, 1)
        cast_s(1, 0)
        quantise_x(0, 1)
        gather_words(0, 0)
        gather_words(0, 1)
        cast_s(1, 1)
        gather_bytes(0, 0)
        cast_v(1, 1)
        quantise_x(1, 0)
        quantise_x(1, 1)
        gather_bytes(0, 1)
        gather_words(1, 0)
        gather_bytes(1, 0)
        first_layer(0, 0)
        gather_bytes(1, 1)
        first_layer(0, 1)
        silu(0)
        first_layer(1, 0)
        gather_words(1, 1)
        first_layer(1, 1)
        silu(1)
        first_layer(2, 0)
        gather_words(0, 2)
        multiply(0)
        gather_bytes(1, 2)
        gather_bytes(0, 2)
        multiply(1)
        turn(0)
        first_layer(2, 1)
        group_h(0)
        first_layer(3, 0)
        quantise_h(0)
        turn(1)
        silu(2)
        second_layer(0)
        gather_words(1, 2)
        first_layer(3, 1)
        group_h(1)
        empty_y(0)
        multiply(2)
        quantise_h(1)
        scatter(0, 0)
        silu(3)
        turn(2)
        group_h(2)
        multiply(3)
        second_layer(1)
        quantise_h(2)
        empty_y(1)
        scatter(0, 1)
        turn(3)
        group_h(3)
        scatter(1, 0)
        scatter(1, 1)
        quantise_h(3)
        second_layer(2)
        scatter(0, 2)
        empty_y(2)
        scatter(1, 2)
        second_layer(3)
        empty_y(3)
        scatter(2, 0)
        scatter(2, 1)
        scatter(2, 2)
        scatter(3, 0)
        scatter(3, 1)
        scatter(3, 2)

        for n in range(N_TILES):
            nc.sync.dma_start(out[n * P : (n + 1) * P, :], out_sb[n][:])
